import numpy as np
import ml_dtypes


def mxq(x, axis, fmt="e4m3"):
    dtype, down = {"e4m3": (ml_dtypes.float8_e4m3fn, 7), "e5m2": (ml_dtypes.float8_e5m2, 14)}[fmt]
    v = np.moveaxis(np.asarray(x, np.float32).astype(ml_dtypes.bfloat16).astype(np.float64), axis, -1)
    blocks = v.reshape(v.shape[:-1] + (-1, 32))
    amax = np.abs(blocks).max(-1, keepdims=True)
    byte = np.maximum(np.where(amax > 0, np.frexp(amax)[1] - 1 + 127, 0) - down, 1)
    scale = np.exp2(byte - 127.0)
    codes = (blocks / scale).astype(np.float32).astype(dtype).astype(np.float64)
    return np.moveaxis((codes * scale).reshape(v.shape), -1, axis)


WIDE = False


def mx_kscale(k):
    if not WIDE:
        return np.ones(k)
    levels = np.array([10, -10, 5, -5, 0])
    if k % 512:
        return np.exp2(np.random.permutation(np.resize(levels, k // 32))).repeat(32)
    a = np.empty((k // 512, 16))
    for p in range(k // 512):
        a[p, :8] = np.random.permutation(np.resize(levels, 8))
        for g in range(8):
            far = levels[np.abs(levels - a[p, g]) >= 10]
            a[p, g + 8] = far[np.random.randint(len(far))]
    return np.exp2(a.ravel()).repeat(32)


def f64(x):
    return np.asarray(x).astype(np.float64)


def striped(idx):
    return np.tile(idx.reshape(-1, 16).T, (8, 1)).astype(np.uint16)


def unstriped(offs):
    return offs[:16].T.reshape(-1).astype(np.int64)


def striped8(idx):
    return np.concatenate([x.reshape(-1, 16).T for x in idx]).astype(np.uint16)


def runs(offs, k):
    lists = np.stack([offs[16 * r : 16 * r + 16].T.reshape(-1) for r in range(8)]).astype(np.int64)
    return lists[np.arange(k) % 512 // 64]


def pack_weight(w):
    k, n = w.shape
    w = f64(np.asarray(w, np.float32).astype(ml_dtypes.bfloat16)).reshape(k // 32, 32, n)
    amax = np.abs(w).max(1)
    byte = np.clip(np.where(amax > 0, np.frexp(amax)[1] - 1 + 127 - 7, 1), 1, 254)
    scaled = (w * np.exp2(127.0 - byte)[:, None, :]).reshape(k, n).astype(np.float32)
    words = np.ascontiguousarray(scaled.reshape(k // 512, 128, 4, n).transpose(0, 1, 3, 2)).astype(ml_dtypes.float8_e4m3fn).view(np.uint8)
    return words, np.ascontiguousarray(byte.astype(np.uint8).reshape(k // 512, 16, n))


def unpack_weight(words, scales):
    g, p, n, _ = words.shape
    vals = np.ascontiguousarray(words).view(ml_dtypes.float8_e4m3fn).astype(np.float64) * np.repeat(np.exp2(scales.astype(np.float64) - 127.0), 8, axis=1)[..., None]
    return vals.transpose(0, 1, 3, 2).reshape(g * 512, n)


def sigmoid(v):
    return 1.0 / (1.0 + np.exp(-np.maximum(v, -700.0)))

def planes(y):
    n, m = y.shape
    v = y.astype(np.float32).astype(ml_dtypes.bfloat16).astype(np.float64).reshape(n // 32, 32, m)
    top = np.abs(v).max(1)
    byte = np.clip(np.where(top > 0, np.frexp(top)[1] - 1 + 127 - 7, 1), 1, 254)
    codes = (v * np.exp2(127.0 - byte)[:, None, :]).reshape(n, m).astype(np.float32).astype(ml_dtypes.float8_e4m3fn).view(np.uint8)
    words = codes.reshape(n // 512, 128, 4, m).transpose(0, 1, 3, 2)
    return np.ascontiguousarray(words), np.ascontiguousarray(byte.astype(np.uint8).reshape(n // 512, 16, m))


K, T, S, N, H, G = 512, 2048, 256, 512, 512, 2048


def setup_inputs():
    n = np.random.standard_normal
    s = mx_kscale(K)[:, None]
    u = mx_kscale(K)
    packed_xT = pack_weight(n((K, T)) * s)
    packed_w1 = pack_weight(n((K, H)) / np.sqrt(K) / s)
    packed_w2 = pack_weight(n((H, N)) / np.sqrt(H) / u[:, None])
    packed_dT = pack_weight(n((K, G)) / s)
    return {
        "x_words": packed_xT[0],
        "x_scales": packed_xT[1],
        "w1_words": packed_w1[0],
        "w1_scales": packed_w1[1],
        "gn": (np.random.uniform(0.5, 1.5, (H, 1)) * u[:, None]).astype(np.float32),
        "w2_words": packed_w2[0],
        "w2_scales": packed_w2[1],
        "d_words": packed_dT[0],
        "d_scales": packed_dT[1],
        "offs": striped(np.random.permutation(T)[:S]),
        "n1": striped(np.random.permutation(S)),
        "n2": striped(np.random.permutation(S)),
        "two": striped(np.random.permutation(T)[:S]),
        "k1": striped8(np.random.randint(0, G, (8, H))),
        "n3": striped8(np.stack([np.random.permutation(S) for _ in range(8)])),
        "n4": striped8(np.stack([np.random.permutation(S) for _ in range(8)])),
    }


def reference(x_words, x_scales, w1_words, w1_scales, gn, w2_words, w2_scales, d_words, d_scales, offs, n1, n2, two, k1, n3, n4):
    xq = unpack_weight(x_words, x_scales)[:, unstriped(offs)]
    y = unpack_weight(w1_words, w1_scales).T @ xq
    sm = np.maximum(y, y[:, unstriped(n2)])
    ds = np.zeros((H, S))
    ds[:, unstriped(n1)] = sm
    z = f64(gn) * (ds * sigmoid(y))
    a = unpack_weight(w2_words, w2_scales).T @ mxq(z, 0, "e4m3")
    d_k1 = unpack_weight(d_words, d_scales)[np.arange(K)[:, None], runs(k1, K)]
    x_two = unpack_weight(x_words, x_scales)[:, unstriped(two)]
    b = 0.0625 * (d_k1.T @ x_two)
    out_0 = np.maximum(a, b[np.arange(H)[:, None], runs(n4, H)]) - (np.minimum(a[np.arange(N)[:, None], runs(n3, N)], b))
    return (out_0,) + planes(out_0)

@@ -1,0 +1,227 @@
+from contextlib import ExitStack
+
+import concourse.mybir as mybir
+
+K, T, S, N, H, G = 512, 2048, 256, 512, 512, 2048
+FLOPS = 2 * K * H * S + 2 * H * N * S + 2 * K * H * S
+
+F32 = mybir.dt.float32
+BF16 = mybir.dt.bfloat16
+I32 = mybir.dt.int32
+U32 = mybir.dt.uint32
+U16 = mybir.dt.uint16
+U8 = mybir.dt.uint8
+FP8X4 = mybir.dt.float8_e4m3fn_x4
+ALU = mybir.AluOpType
+ACT = mybir.ActivationFunctionType
+
+P = 128
+PACK = 4
+PAD = 16
+
+
+def words_in_hbm(words):
+    return words[0].rearrange("p n t -> p (n t)").bitcast(I32)
+
+
+def load_scale_rows(queues, plane, scales):
+    rows = scales[0].bitcast(I32)
+    for q, queue in enumerate(queues):
+        queue.dma_start(plane[32 * q : 32 * q + 4, :].bitcast(I32), rows[4 * q : 4 * q + 4, :])
+
+
+def deal_words(nc, dealt, plain):
+    nc.vector.tensor_copy(
+        dealt[:].rearrange("p (t c i) -> p c t i", t=PACK, i=4),
+        plain[:].rearrange("p (c i t) -> p c t i", t=PACK, i=4),
+    )
+
+
+def deal_bytes(nc, dealt, plain):
+    nc.vector.tensor_copy(
+        dealt[:].rearrange("p (t m) -> p t m", t=PACK),
+        plain[:].rearrange("p (m t) -> p t m", t=PACK),
+    )
+
+
+def product(nc, bank, t, w_words, w_scales, x_words, x_scales):
+    cols = slice(t * P, (t + 1) * P)
+    nc.tensor.matmul_mx(
+        out=bank[:],
+        lhsT=w_words[:, cols].bitcast(FP8X4),
+        lhsT_scale=w_scales[:, cols],
+        rhs=x_words[:].bitcast(FP8X4),
+        rhs_scale=x_scales[:],
+        start=True,
+        stop=True,
+    )
+
+
+def round_pair(nc, grouped, planes, first):
+    nc.vector.tensor_copy(
+        grouped[:, :, first : first + 2],
+        planes[:, first : first + 2, :].rearrange("p t c -> p c t"),
+    )
+
+
+def tile_picked_cdjoinmaxbsendg_none_po_kernel(
+    tc, x_words, x_scales, w1_words, w1_scales, gn, w2_words, w2_scales, d_words, d_scales,
+    offs, n1, n2, two, k1, n3, n4, out_0, out_1, out_2,
+):
+    nc = tc.nc
+    with ExitStack() as ctx:
+        sb = ctx.enter_context(tc.tile_pool(name="sb", bufs=1))
+        psum = ctx.enter_context(tc.psum_pool(name="psum", bufs=1))
+
+        def tile(name, shape, dtype, tag=None):
+            return sb.tile(shape, dtype, name=name, tag=tag or name, align_bytes=64)
+
+        def load_list(name, src):
+            lst = tile(name, list(src.shape), U16)
+            nc.sync.dma_start(lst[:], src)
+            return lst
+
+        xw = tile("xw", [P, T], U32)
+        xs = tile("xs", [P, T], U8)
+        dw = tile("dw", [P, G], U32)
+        dsc = tile("dsc", [P, G], U8)
+        w1w = tile("w1w", [P, H], U32)
+        w1s = tile("w1s", [P, H], U8)
+        d_plane = tile("d_plane", [P, H], U8)
+        gain = tile("gain", [P, PACK], F32)
+        y = [tile(f"y{t}", [P, S + PAD], F32) for t in range(PACK)]
+
+        nc.vector.memset(xs[:].bitcast(I32), 0)
+        nc.vector.memset(w1s[:].bitcast(I32), 0)
+        nc.vector.memset(dsc[:].bitcast(I32), 0)
+        nc.vector.memset(d_plane[:].bitcast(I32), 0)
+        for t in range(PACK):
+            nc.vector.memset(y[t][:, S:], 0.0)
+
+        offs_t = load_list("offs_t", offs)
+        n2_t = load_list("n2_t", n2)
+        nc.sync.dma_start(w1w[:].bitcast(I32), words_in_hbm(w1_words))
+        nc.sync.dma_start(xw[:].bitcast(I32), words_in_hbm(x_words))
+        nc.sync.dma_start(dw[:].bitcast(I32), words_in_hbm(d_words))
+        nc.sync.dma_start(dsc[0:P:8, :].bitcast(I32), d_scales[0].bitcast(I32))
+        k1_t = load_list("k1_t", k1)
+        two_t = load_list("two_t", two)
+        n1_t = load_list("n1_t", n1)
+        nc.sync.dma_start(gain[:], gn.rearrange("(p t) o -> p (t o)", t=PACK))
+        n4_t = load_list("n4_t", n4)
+        n3_t = load_list("n3_t", n3)
+        load_scale_rows([nc.scalar] * 4, xs, x_scales)
+        load_scale_rows([nc.scalar] * 3 + [nc.gpsimd], w1s, w1_scales)
+
+        xq_s = tile("xq_s", [P, S], U8)
+        xq_w = tile("xq_w", [P, S], U32)
+        w1w_d = tile("w1w_d", [P, H], U32)
+        w1s_d = tile("w1s_d", [P, H], U8)
+        nc.vector.tensor_copy(xq_s[:], xs[:].indirect(offs_t[:]))
+        deal_words(nc, w1w_d, w1w)
+        deal_bytes(nc, w1s_d, w1s)
+        nc.vector.tensor_copy(xq_w[:], xw[:].indirect(offs_t[:]))
+
+        y_bank = [psum.tile([P, S], F32, name=f"y_bank{t}", tag=f"bank{t}") for t in range(PACK)]
+        last = PACK - 1
+        for t in [last] + list(range(last)):
+            product(nc, y_bank[t], t, w1w_d, w1s_d, xq_w, xq_s)
+
+        b_sig = [tile(f"b_sig{t}", [P, 2 * S], F32) for t in range(PACK)]
+        a_bg = [tile(f"a_bg{t}", [P, 2 * S], F32) for t in range(PACK)]
+        yg = tile("yg", [P, PACK, S], F32)
+        sm_early = tile("sm_early", [P, 2, S], F32)
+        ds = [tile(f"ds{t}", [P, 2 * S], F32) for t in range(PACK)]
+        z = tile("z", [P, PACK, S], F32)
+        zb = tile("zb", [P, S, PACK], BF16)
+
+        nc.scalar.activation(b_sig[last][:, S:], y_bank[last][:], ACT.Sigmoid)
+        for t in range(PACK):
+            nc.vector.tensor_copy(y[t][:, :S], y_bank[t][:])
+            nc.scalar.activation(yg[:, t, :], y[t][:].indirect(n2_t[:]), ACT.Copy)
+
+        def larger(sm, first):
+            for u in range(2):
+                nc.vector.tensor_tensor(sm[:, u, :], y[first + u][:, :S], yg[:, first + u, :], ALU.max)
+
+        def send(sm, first):
+            for u in range(2):
+                nc.scalar.activation(ds[first + u][:].indirect(n1_t[:]), sm[:, u, :], ACT.Copy)
+
+        larger(sm_early, 0)
+        send(sm_early, 0)
+        for t in range(last):
+            nc.scalar.activation(b_sig[t][:, S:], y[t][:, :S], ACT.Sigmoid)
+
+        dq_s = tile("dq_s", [P, H], U8)
+        dq_s_d = tile("dq_s_d", [P, H], U8, tag="late")
+        dq_w = tile("dq_w", [P, H], U32)
+        dq_w_d = tile("dq_w_d", [P, H], U32)
+        x2_s = tile("x2_s", [P, S], U8)
+        x2_w = tile("x2_w", [P, S], U32)
+        nc.vector.tensor_copy(dq_s[:], dsc[:].indirect(k1_t[:]))
+        nc.vector.tensor_copy(x2_s[:], xs[:].indirect(two_t[:]))
+        deal_bytes(nc, dq_s_d, dq_s)
+        for s in range(4):
+            nc.sync.dma_start(d_plane[s:P:32, :].bitcast(I32), dq_s_d[8 * s : P : 32, :].bitcast(I32))
+        sm_late = tile("sm_late", [P, 2, S], F32, tag="late")
+        larger(sm_late, 2)
+        send(sm_late, 2)
+        nc.vector.tensor_copy(dq_w[:], dw[:].indirect(k1_t[:]))
+        nc.vector.tensor_copy(x2_w[:], xw[:].indirect(two_t[:]))
+        deal_words(nc, dq_w_d, dq_w)
+        w2w_d = tile("w2w_d", [P, N], U32)
+        w2s_d = tile("w2s_d", [P, N], U8)
+        nc.sync.dma_start(w1w[:].bitcast(I32), words_in_hbm(w2_words))
+        load_scale_rows([nc.sync] * 4, w1s, w2_scales)
+        deal_words(nc, w2w_d, w1w)
+        deal_bytes(nc, w2s_d, w1s)
+        for t in range(PACK):
+            b_bank = psum.tile([P, S], F32, name=f"b_bank{t}")
+            product(nc, b_bank, t, dq_w_d, d_plane, x2_w, x2_s)
+            nc.vector.tensor_scalar_mul(b_sig[t][:, :S], b_bank[:], 0.0625)
+
+        for t in range(PACK):
+            nc.vector.scalar_tensor_tensor(
+                z[:, t, :], ds[t][:, :S], gain[:, t : t + 1], b_sig[t][:, S:], ALU.mult, ALU.mult
+            )
+            if t % 2 == 1:
+                round_pair(nc, zb, z, t - 1)
+        zw = tile("zw", [P, S], U32)
+        zs = tile("zs", [P, S], U8)
+        nc.vector.quantize_mx(zw[:].bitcast(FP8X4), zs[:], zb[:].rearrange("p c t -> p (c t)"))
+
+        for t in range(PACK):
+            nc.scalar.activation(a_bg[t][:, S:], b_sig[t][:].indirect(n4_t[:]), ACT.Copy)
+
+        a_bank = [psum.tile([P, S], F32, name=f"a_bank{t}", tag=f"bank{t}") for t in range(PACK)]
+        for t in range(PACK):
+            product(nc, a_bank[t], t, w2w_d, w2s_d, zw, zs)
+
+        hi = tile("hi", [P, PACK, S], F32)
+        lo = tile("lo", [P, PACK, S], F32)
+        ag = tile("ag", [P, PACK, S], F32)
+        res = tile("res", [P, PACK, S], F32)
+        rb = tile("rb", [P, S, PACK], BF16)
+        out_rows = out_0.rearrange("(p t) c -> p t c", t=PACK)
+
+        nc.scalar.activation(a_bg[0][:, :S], a_bank[0][:], ACT.Copy)
+        for t in [1, 2, 3, 0]:
+            nc.vector.tensor_tensor(hi[:, t, :], a_bank[t][:], a_bg[t][:, S:], ALU.max)
+        for t in range(PACK):
+            if t > 0:
+                nc.scalar.activation(a_bg[t][:, :S], a_bank[t][:], ACT.Copy)
+            nc.scalar.activation(ag[:, t, :], a_bg[t][:].indirect(n3_t[:]), ACT.Copy)
+            nc.vector.tensor_tensor(lo[:, t, :], ag[:, t, :], b_sig[t][:, :S], ALU.min)
+            nc.vector.tensor_tensor(res[:, t, :], hi[:, t, :], lo[:, t, :], ALU.subtract)
+            nc.sync.dma_start(out_rows[:, t, :], res[:, t, :])
+            if t % 2 == 1:
+                round_pair(nc, rb, res, t - 1)
+        ow = tile("ow", [P, S], U32)
+        os_ = tile("os_", [P, S], U8)
+        nc.vector.quantize_mx(ow[:].bitcast(FP8X4), os_[:], rb[:].rearrange("p c t -> p (c t)"))
+        nc.sync.dma_start(words_in_hbm(out_1), ow[:].bitcast(I32))
+        rows = out_2[0].bitcast(I32)
+        for q in range(4):
+            queue = nc.scalar if q < 2 else nc.sync
+            queue.dma_start(rows[4 * q : 4 * q + 4, :], os_[32 * q : 32 * q + 4, :].bitcast(I32))

@@ -18,6 +18,8 @@ ACT = mybir.ActivationFunctionType
 P = 128
 PACK = 4
 PAD = 16
+ALL = slice(0, S)
+HALVES = (slice(0, S // 2), slice(S // 2, S))
 
 
 def words_in_hbm(words):
@@ -44,23 +46,29 @@ def deal_bytes(nc, dealt, plain):
     )
 
 
-def product(nc, bank, t, w_words, w_scales, x_words, x_scales):
+def product(nc, bank, t, w_words, w_scales, x_words, x_scales, places=slice(0, S)):
     cols = slice(t * P, (t + 1) * P)
     nc.tensor.matmul_mx(
-        out=bank[:],
+        out=bank[:, places],
         lhsT=w_words[:, cols].bitcast(FP8X4),
         lhsT_scale=w_scales[:, cols],
-        rhs=x_words[:].bitcast(FP8X4),
-        rhs_scale=x_scales[:],
+        rhs=x_words[:, places].bitcast(FP8X4),
+        rhs_scale=x_scales[:, places],
         start=True,
         stop=True,
     )
 
 
-def round_pair(nc, grouped, planes, first):
-    nc.vector.tensor_copy(
-        grouped[:, :, first : first + 2],
-        planes[:, first : first + 2, :].rearrange("p t c -> p c t"),
+def round_pair(copy, grouped, planes, first, cols):
+    copy(
+        grouped[:, cols, first : first + 2],
+        planes[:, first : first + 2, cols].rearrange("p t c -> p c t"),
+    )
+
+
+def quantise(nc, words, scales, grouped, cols):
+    nc.vector.quantize_mx(
+        words[:, cols].bitcast(FP8X4), scales[:, cols], grouped[:, cols, :].rearrange("p c t -> p (c t)")
     )
 
 
@@ -99,19 +107,16 @@ def tile_picked_cdjoinmaxbsendg_none_po_kernel(
             nc.vector.memset(y[t][:, S:], 0.0)
 
         offs_t = load_list("offs_t", offs)
-        n2_t = load_list("n2_t", n2)
         nc.sync.dma_start(w1w[:].bitcast(I32), words_in_hbm(w1_words))
+        load_scale_rows([nc.sync] * 2 + [nc.scalar] * 2, xs, x_scales)
         nc.sync.dma_start(xw[:].bitcast(I32), words_in_hbm(x_words))
-        nc.sync.dma_start(dw[:].bitcast(I32), words_in_hbm(d_words))
+        load_scale_rows([nc.scalar] * 4, w1s, w1_scales)
+        n2_t = load_list("n2_t", n2)
         nc.sync.dma_start(dsc[0:P:8, :].bitcast(I32), d_scales[0].bitcast(I32))
         k1_t = load_list("k1_t", k1)
         two_t = load_list("two_t", two)
+        nc.sync.dma_start(dw[:].bitcast(I32), words_in_hbm(d_words))
         n1_t = load_list("n1_t", n1)
-        nc.sync.dma_start(gain[:], gn.rearrange("(p t) o -> p (t o)", t=PACK))
-        n4_t = load_list("n4_t", n4)
-        n3_t = load_list("n3_t", n3)
-        load_scale_rows([nc.scalar] * 4, xs, x_scales)
-        load_scale_rows([nc.scalar] * 3 + [nc.gpsimd], w1s, w1_scales)
 
         xq_s = tile("xq_s", [P, S], U8)
         xq_w = tile("xq_w", [P, S], U32)
@@ -119,18 +124,18 @@ def tile_picked_cdjoinmaxbsendg_none_po_kernel(
         w1s_d = tile("w1s_d", [P, H], U8)
         nc.vector.tensor_copy(xq_s[:], xs[:].indirect(offs_t[:]))
         deal_words(nc, w1w_d, w1w)
-        deal_bytes(nc, w1s_d, w1s)
         nc.vector.tensor_copy(xq_w[:], xw[:].indirect(offs_t[:]))
+        deal_bytes(nc, w1s_d, w1s)
 
         y_bank = [psum.tile([P, S], F32, name=f"y_bank{t}", tag=f"bank{t}") for t in range(PACK)]
         last = PACK - 1
-        for t in [last] + list(range(last)):
+        for t in (0, last, 1, 2):
             product(nc, y_bank[t], t, w1w_d, w1s_d, xq_w, xq_s)
 
         b_sig = [tile(f"b_sig{t}", [P, 2 * S], F32) for t in range(PACK)]
         a_bg = [tile(f"a_bg{t}", [P, 2 * S], F32) for t in range(PACK)]
-        yg = tile("yg", [P, PACK, S], F32)
-        sm_early = tile("sm_early", [P, 2, S], F32)
+        yg = [tile(f"yg{t}", [P, S], F32) for t in range(PACK)]
+        sm = tile("sm", [P, PACK, S], F32)
         ds = [tile(f"ds{t}", [P, 2 * S], F32) for t in range(PACK)]
         z = tile("z", [P, PACK, S], F32)
         zb = tile("zb", [P, S, PACK], BF16)
@@ -138,42 +143,39 @@ def tile_picked_cdjoinmaxbsendg_none_po_kernel(
         nc.scalar.activation(b_sig[last][:, S:], y_bank[last][:], ACT.Sigmoid)
         for t in range(PACK):
             nc.vector.tensor_copy(y[t][:, :S], y_bank[t][:])
-            nc.scalar.activation(yg[:, t, :], y[t][:].indirect(n2_t[:]), ACT.Copy)
-
-        def larger(sm, first):
-            for u in range(2):
-                nc.vector.tensor_tensor(sm[:, u, :], y[first + u][:, :S], yg[:, first + u, :], ALU.max)
-
-        def send(sm, first):
-            for u in range(2):
-                nc.scalar.activation(ds[first + u][:].indirect(n1_t[:]), sm[:, u, :], ACT.Copy)
-
-        larger(sm_early, 0)
-        send(sm_early, 0)
+        for t in range(last):
+            nc.scalar.activation(yg[t][:], y[t][:].indirect(n2_t[:]), ACT.Copy)
         for t in range(last):
             nc.scalar.activation(b_sig[t][:, S:], y[t][:, :S], ACT.Sigmoid)
+        nc.scalar.activation(yg[last][:], y[last][:].indirect(n2_t[:]), ACT.Copy)
 
         dq_s = tile("dq_s", [P, H], U8)
-        dq_s_d = tile("dq_s_d", [P, H], U8, tag="late")
-        dq_w = tile("dq_w", [P, H], U32)
-        dq_w_d = tile("dq_w_d", [P, H], U32)
-        x2_s = tile("x2_s", [P, S], U8)
-        x2_w = tile("x2_w", [P, S], U32)
+        dq_s_d = tile("dq_s_d", [P, H], U8)
         nc.vector.tensor_copy(dq_s[:], dsc[:].indirect(k1_t[:]))
-        nc.vector.tensor_copy(x2_s[:], xs[:].indirect(two_t[:]))
         deal_bytes(nc, dq_s_d, dq_s)
         for s in range(4):
             nc.sync.dma_start(d_plane[s:P:32, :].bitcast(I32), dq_s_d[8 * s : P : 32, :].bitcast(I32))
-        sm_late = tile("sm_late", [P, 2, S], F32, tag="late")
-        larger(sm_late, 2)
-        send(sm_late, 2)
-        nc.vector.tensor_copy(dq_w[:], dw[:].indirect(k1_t[:]))
+        nc.sync.dma_start(w1w[:].bitcast(I32), words_in_hbm(w2_words))
+        load_scale_rows([nc.sync] * 4, w1s, w2_scales)
+        nc.sync.dma_start(gain[:], gn.rearrange("(p t) o -> p (t o)", t=PACK))
+        n4_t = load_list("n4_t", n4)
+        n3_t = load_list("n3_t", n3)
+
+        for t in range(PACK):
+            nc.vector.tensor_tensor(sm[:, t, :], y[t][:, :S], yg[t][:], ALU.max)
+        for t in range(PACK):
+            nc.scalar.activation(ds[t][:].indirect(n1_t[:]), sm[:, t, :], ACT.Copy)
+
+        dq_w = tile("dq_w", [P, H], U32, tag="yg2")
+        dq_w_d = tile("dq_w_d", [P, H], U32)
+        x2_s = tile("x2_s", [P, S], U8, tag="yg1")
+        x2_w = tile("x2_w", [P, S], U32, tag="yg0")
+        nc.vector.tensor_copy(x2_s[:], xs[:].indirect(two_t[:]))
         nc.vector.tensor_copy(x2_w[:], xw[:].indirect(two_t[:]))
+        nc.vector.tensor_copy(dq_w[:], dw[:].indirect(k1_t[:]))
         deal_words(nc, dq_w_d, dq_w)
         w2w_d = tile("w2w_d", [P, N], U32)
         w2s_d = tile("w2s_d", [P, N], U8)
-        nc.sync.dma_start(w1w[:].bitcast(I32), words_in_hbm(w2_words))
-        load_scale_rows([nc.sync] * 4, w1s, w2_scales)
         deal_words(nc, w2w_d, w1w)
         deal_bytes(nc, w2s_d, w1s)
         for t in range(PACK):
@@ -181,45 +183,84 @@ def tile_picked_cdjoinmaxbsendg_none_po_kernel(
             product(nc, b_bank, t, dq_w_d, d_plane, x2_w, x2_s)
             nc.vector.tensor_scalar_mul(b_sig[t][:, :S], b_bank[:], 0.0625)
 
-        for t in range(PACK):
+        def gated(t, cols):
             nc.vector.scalar_tensor_tensor(
-                z[:, t, :], ds[t][:, :S], gain[:, t : t + 1], b_sig[t][:, S:], ALU.mult, ALU.mult
+                z[:, t, cols], ds[t][:, cols], gain[:, t : t + 1], b_sig[t][:, S:][:, cols], ALU.mult, ALU.mult
             )
-            if t % 2 == 1:
-                round_pair(nc, zb, z, t - 1)
+
         zw = tile("zw", [P, S], U32)
         zs = tile("zs", [P, S], U8)
-        nc.vector.quantize_mx(zw[:].bitcast(FP8X4), zs[:], zb[:].rearrange("p c t -> p (c t)"))
+        gated(0, ALL)
+        gated(1, ALL)
+        round_pair(nc.vector.tensor_copy, zb, z, 0, ALL)
+        gated(2, ALL)
+        for cols in HALVES:
+            gated(3, cols)
+        for cols in HALVES:
+            round_pair(nc.vector.tensor_copy, zb, z, 2, cols)
+        for cols in HALVES:
+            quantise(nc, zw, zs, zb, cols)
 
         for t in range(PACK):
             nc.scalar.activation(a_bg[t][:, S:], b_sig[t][:].indirect(n4_t[:]), ACT.Copy)
 
         a_bank = [psum.tile([P, S], F32, name=f"a_bank{t}", tag=f"bank{t}") for t in range(PACK)]
-        for t in range(PACK):
-            product(nc, a_bank[t], t, w2w_d, w2s_d, zw, zs)
+        for cols in HALVES:
+            for t in range(PACK):
+                product(nc, a_bank[t], t, w2w_d, w2s_d, zw, zs, cols)
 
         hi = tile("hi", [P, PACK, S], F32)
         lo = tile("lo", [P, PACK, S], F32)
         ag = tile("ag", [P, PACK, S], F32)
         res = tile("res", [P, PACK, S], F32)
         rb = tile("rb", [P, S, PACK], BF16)
-        out_rows = out_0.rearrange("(p t) c -> p t c", t=PACK)
-
-        nc.scalar.activation(a_bg[0][:, :S], a_bank[0][:], ACT.Copy)
-        for t in [1, 2, 3, 0]:
-            nc.vector.tensor_tensor(hi[:, t, :], a_bank[t][:], a_bg[t][:, S:], ALU.max)
-        for t in range(PACK):
-            if t > 0:
-                nc.scalar.activation(a_bg[t][:, :S], a_bank[t][:], ACT.Copy)
-            nc.scalar.activation(ag[:, t, :], a_bg[t][:].indirect(n3_t[:]), ACT.Copy)
-            nc.vector.tensor_tensor(lo[:, t, :], ag[:, t, :], b_sig[t][:, :S], ALU.min)
-            nc.vector.tensor_tensor(res[:, t, :], hi[:, t, :], lo[:, t, :], ALU.subtract)
-            nc.sync.dma_start(out_rows[:, t, :], res[:, t, :])
-            if t % 2 == 1:
-                round_pair(nc, rb, res, t - 1)
         ow = tile("ow", [P, S], U32)
         os_ = tile("os_", [P, S], U8)
-        nc.vector.quantize_mx(ow[:].bitcast(FP8X4), os_[:], rb[:].rearrange("p c t -> p (c t)"))
+        out_rows = out_0.rearrange("(p t) c -> p t c", t=PACK)
+
+        def leave_bank(t):
+            nc.scalar.activation(a_bg[t][:, :S], a_bank[t][:], ACT.Copy)
+
+        def fetch(t, cols):
+            entries = n3_t[:, cols.start // 16 : cols.stop // 16]
+            nc.scalar.activation(ag[:, t, cols], a_bg[t][:].indirect(entries), ACT.Copy)
+
+        def larger(t):
+            nc.vector.tensor_tensor(hi[:, t, :], a_bank[t][:], a_bg[t][:, S:], ALU.max)
+
+        def smaller(t, cols):
+            nc.vector.tensor_tensor(lo[:, t, cols], ag[:, t, cols], b_sig[t][:, cols], ALU.min)
+
+        def less(t, cols):
+            nc.vector.tensor_tensor(res[:, t, cols], hi[:, t, cols], lo[:, t, cols], ALU.subtract)
+
+        leave_bank(0)
+        leave_bank(1)
+        larger(2)
+        larger(3)
+        fetch(0, ALL)
+        leave_bank(2)
+        fetch(1, ALL)
+        leave_bank(3)
+        for cols in HALVES:
+            fetch(2, cols)
+            fetch(3, cols)
+        larger(0)
+        smaller(0, ALL)
+        larger(1)
+        less(0, ALL)
+        smaller(1, ALL)
+        less(1, ALL)
+        nc.sync.dma_start(out_rows[:, 0:2, :], res[:, 0:2, :])
+        round_pair(nc.scalar.copy, rb, res, 0, ALL)
+        for cols in HALVES:
+            smaller(2, cols)
+            smaller(3, cols)
+            less(2, cols)
+            less(3, cols)
+            round_pair(nc.vector.tensor_copy, rb, res, 2, cols)
+            quantise(nc, ow, os_, rb, cols)
+        nc.sync.dma_start(out_rows[:, 2:4, :], res[:, 2:4, :])
         nc.sync.dma_start(words_in_hbm(out_1), ow[:].bitcast(I32))
         rows = out_2[0].bitcast(I32)
         for q in range(4):

@@ -32,6 +32,11 @@ def load_scale_rows(queues, plane, scales):
         queue.dma_start(plane[32 * q : 32 * q + 4, :].bitcast(I32), rows[4 * q : 4 * q + 4, :])
 
 
+def close_up(queues, plane, apart):
+    for s, queue in enumerate(queues):
+        queue.dma_start(plane[s:P:32, :].bitcast(I32), apart[8 * s : P : 32, :].bitcast(I32))
+
+
 def deal_words(nc, dealt, plain):
     nc.vector.tensor_copy(
         dealt[:].rearrange("p (t c i) -> p c t i", t=PACK, i=4),
@@ -39,10 +44,10 @@ def deal_words(nc, dealt, plain):
     )
 
 
-def deal_bytes(nc, dealt, plain):
+def deal_bytes(nc, dealt, plain, tiles=slice(0, PACK)):
     nc.vector.tensor_copy(
-        dealt[:].rearrange("p (t m) -> p t m", t=PACK),
-        plain[:].rearrange("p (m t) -> p t m", t=PACK),
+        dealt[:].rearrange("p (t m) -> p t m", t=PACK)[:, tiles, :],
+        plain[:].rearrange("p (m t) -> p t m", t=PACK)[:, tiles, :],
     )
 
 
@@ -99,38 +104,41 @@ def tile_picked_cdjoinmaxbsendg_none_po_kernel(
         gain = tile("gain", [P, PACK], F32)
         y = [tile(f"y{t}", [P, S + PAD], F32) for t in range(PACK)]
 
-        nc.vector.memset(xs[:].bitcast(I32), 0)
-        nc.vector.memset(w1s[:].bitcast(I32), 0)
-        nc.vector.memset(dsc[:].bitcast(I32), 0)
-        nc.vector.memset(d_plane[:].bitcast(I32), 0)
+        xs_apart = tile("xs_apart", [P, T], U8)
+        xq_plane = tile("xq_plane", [P, S], U8)
+        for plane in (w1s, xs_apart, xq_plane, dsc, xs, d_plane):
+            nc.vector.memset(plane[:].bitcast(I32), 0)
         for t in range(PACK):
             nc.vector.memset(y[t][:, S:], 0.0)
 
         offs_t = load_list("offs_t", offs)
         nc.sync.dma_start(w1w[:].bitcast(I32), words_in_hbm(w1_words))
-        load_scale_rows([nc.sync] * 2 + [nc.scalar] * 2, xs, x_scales)
+        nc.sync.dma_start(xs_apart[0:P:8, :].bitcast(I32), x_scales[0].bitcast(I32))
         nc.sync.dma_start(xw[:].bitcast(I32), words_in_hbm(x_words))
         load_scale_rows([nc.scalar] * 4, w1s, w1_scales)
         n2_t = load_list("n2_t", n2)
-        nc.sync.dma_start(dsc[0:P:8, :].bitcast(I32), d_scales[0].bitcast(I32))
-        k1_t = load_list("k1_t", k1)
-        two_t = load_list("two_t", two)
-        nc.sync.dma_start(dw[:].bitcast(I32), words_in_hbm(d_words))
-        n1_t = load_list("n1_t", n1)
 
         xq_s = tile("xq_s", [P, S], U8)
         xq_w = tile("xq_w", [P, S], U32)
-        w1w_d = tile("w1w_d", [P, H], U32)
+        nc.vector.tensor_copy(xq_s[:], xs_apart[:].indirect(offs_t[:]))
+        close_up([nc.scalar, nc.sync] * 2, xq_plane, xq_s)
+        w1w_d = tile("w1w_d", [P, H], U32, tag="xs_apart")
         w1s_d = tile("w1s_d", [P, H], U8)
-        nc.vector.tensor_copy(xq_s[:], xs[:].indirect(offs_t[:]))
         deal_words(nc, w1w_d, w1w)
-        nc.vector.tensor_copy(xq_w[:], xw[:].indirect(offs_t[:]))
         deal_bytes(nc, w1s_d, w1s)
+        nc.vector.tensor_copy(xq_w[:], xw[:].indirect(offs_t[:]))
+
+        two_t = load_list("two_t", two)
+        nc.sync.dma_start(dsc[0:P:8, :].bitcast(I32), d_scales[0].bitcast(I32))
+        k1_t = load_list("k1_t", k1)
+        nc.sync.dma_start(dw[:].bitcast(I32), words_in_hbm(d_words))
+        n1_t = load_list("n1_t", n1)
+        load_scale_rows([nc.sync] * 4, xs, x_scales)
 
         y_bank = [psum.tile([P, S], F32, name=f"y_bank{t}", tag=f"bank{t}") for t in range(PACK)]
         last = PACK - 1
         for t in (0, last, 1, 2):
-            product(nc, y_bank[t], t, w1w_d, w1s_d, xq_w, xq_s)
+            product(nc, y_bank[t], t, w1w_d, w1s_d, xq_w, xq_plane)
 
         b_sig = [tile(f"b_sig{t}", [P, 2 * S], F32) for t in range(PACK)]
         a_bg = [tile(f"a_bg{t}", [P, 2 * S], F32) for t in range(PACK)]
@@ -153,8 +161,7 @@ def tile_picked_cdjoinmaxbsendg_none_po_kernel(
         dq_s_d = tile("dq_s_d", [P, H], U8)
         nc.vector.tensor_copy(dq_s[:], dsc[:].indirect(k1_t[:]))
         deal_bytes(nc, dq_s_d, dq_s)
-        for s in range(4):
-            nc.sync.dma_start(d_plane[s:P:32, :].bitcast(I32), dq_s_d[8 * s : P : 32, :].bitcast(I32))
+        close_up([nc.sync] * 4, d_plane, dq_s_d)
         nc.sync.dma_start(w1w[:].bitcast(I32), words_in_hbm(w2_words))
         load_scale_rows([nc.sync] * 4, w1s, w2_scales)
         nc.sync.dma_start(gain[:], gn.rearrange("(p t) o -> p (t o)", t=PACK))
@@ -178,10 +185,10 @@ def tile_picked_cdjoinmaxbsendg_none_po_kernel(
         w2s_d = tile("w2s_d", [P, N], U8)
         deal_words(nc, w2w_d, w1w)
         deal_bytes(nc, w2s_d, w1s)
+        b_bank = [psum.tile([P, S], F32, name=f"b_bank{t}") for t in range(PACK)]
         for t in range(PACK):
-            b_bank = psum.tile([P, S], F32, name=f"b_bank{t}")
-            product(nc, b_bank, t, dq_w_d, d_plane, x2_w, x2_s)
-            nc.vector.tensor_scalar_mul(b_sig[t][:, :S], b_bank[:], 0.0625)
+            product(nc, b_bank[t], t, dq_w_d, d_plane, x2_w, x2_s)
+            nc.vector.tensor_scalar_mul(b_sig[t][:, :S], b_bank[t][:], 0.0625)
 
         def gated(t, cols):
             nc.vector.scalar_tensor_tensor(
@@ -201,13 +208,18 @@ def tile_picked_cdjoinmaxbsendg_none_po_kernel(
         for cols in HALVES:
             quantise(nc, zw, zs, zb, cols)
 
-        for t in range(PACK):
+        def fetch_b(t):
             nc.scalar.activation(a_bg[t][:, S:], b_sig[t][:].indirect(n4_t[:]), ACT.Copy)
+
+        for t in range(PACK):
+            fetch_b(t)
 
         a_bank = [psum.tile([P, S], F32, name=f"a_bank{t}", tag=f"bank{t}") for t in range(PACK)]
         for cols in HALVES:
-            for t in range(PACK):
+            for t in (0, 1):
                 product(nc, a_bank[t], t, w2w_d, w2s_d, zw, zs, cols)
+        for t in (2, 3):
+            product(nc, a_bank[t], t, w2w_d, w2s_d, zw, zs)
 
         hi = tile("hi", [P, PACK, S], F32)
         lo = tile("lo", [P, PACK, S], F32)
@@ -217,11 +229,12 @@ def tile_picked_cdjoinmaxbsendg_none_po_kernel(
         ow = tile("ow", [P, S], U32)
         os_ = tile("os_", [P, S], U8)
         out_rows = out_0.rearrange("(p t) c -> p t c", t=PACK)
+        first, second = HALVES
 
-        def leave_bank(t):
-            nc.scalar.activation(a_bg[t][:, :S], a_bank[t][:], ACT.Copy)
+        def leave_bank(copy, t):
+            copy(a_bg[t][:, :S], a_bank[t][:])
 
-        def fetch(t, cols):
+        def fetch_a(t, cols):
             entries = n3_t[:, cols.start // 16 : cols.stop // 16]
             nc.scalar.activation(ag[:, t, cols], a_bg[t][:].indirect(entries), ACT.Copy)
 
@@ -229,25 +242,23 @@ def tile_picked_cdjoinmaxbsendg_none_po_kernel(
             nc.vector.tensor_tensor(hi[:, t, :], a_bank[t][:], a_bg[t][:, S:], ALU.max)
 
         def smaller(t, cols):
-            nc.vector.tensor_tensor(lo[:, t, cols], ag[:, t, cols], b_sig[t][:, cols], ALU.min)
+            nc.vector.scalar_tensor_tensor(lo[:, t, cols], b_bank[t][:, cols], 0.0625, ag[:, t, cols], ALU.mult, ALU.min)
 
-        def less(t, cols):
-            nc.vector.tensor_tensor(res[:, t, cols], hi[:, t, cols], lo[:, t, cols], ALU.subtract)
+        def less(t, cols, engine=nc.vector):
+            engine.tensor_tensor(res[:, t, cols], hi[:, t, cols], lo[:, t, cols], ALU.subtract)
 
-        leave_bank(0)
-        leave_bank(1)
-        larger(2)
-        larger(3)
-        fetch(0, ALL)
-        leave_bank(2)
-        fetch(1, ALL)
-        leave_bank(3)
+        for t in range(last):
+            leave_bank(nc.vector.tensor_copy, t)
+        fetch_a(0, ALL)
+        leave_bank(nc.scalar.copy, last)
+        fetch_a(1, ALL)
         for cols in HALVES:
-            fetch(2, cols)
-            fetch(3, cols)
-        larger(0)
+            fetch_a(2, cols)
+            fetch_a(3, cols)
+        for t in range(last):
+            larger(t)
         smaller(0, ALL)
-        larger(1)
+        larger(last)
         less(0, ALL)
         smaller(1, ALL)
         less(1, ALL)
@@ -258,10 +269,11 @@ def tile_picked_cdjoinmaxbsendg_none_po_kernel(
             smaller(3, cols)
             less(2, cols)
             less(3, cols)
+            nc.sync.dma_start(out_rows[:, 2:4, cols], res[:, 2:4, cols])
             round_pair(nc.vector.tensor_copy, rb, res, 2, cols)
+        for cols in HALVES:
             quantise(nc, ow, os_, rb, cols)
-        nc.sync.dma_start(out_rows[:, 2:4, :], res[:, 2:4, :])
-        nc.sync.dma_start(words_in_hbm(out_1), ow[:].bitcast(I32))
+            nc.sync.dma_start(words_in_hbm(out_1)[:, cols], ow[:, cols].bitcast(I32))
         rows = out_2[0].bitcast(I32)
         for q in range(4):
             queue = nc.scalar if q < 2 else nc.sync

from contextlib import ExitStack

import concourse.mybir as mybir

K, T, S, N, H, G = 512, 2048, 256, 512, 512, 2048
FLOPS = 2 * K * H * S + 2 * H * N * S + 2 * K * H * S

F32 = mybir.dt.float32
BF16 = mybir.dt.bfloat16
I32 = mybir.dt.int32
U32 = mybir.dt.uint32
U16 = mybir.dt.uint16
U8 = mybir.dt.uint8
FP8X4 = mybir.dt.float8_e4m3fn_x4
ALU = mybir.AluOpType
ACT = mybir.ActivationFunctionType

P = 128
PACK = 4
PAD = 16
ALL = slice(0, S)
HALVES = (slice(0, S // 2), slice(S // 2, S))


def words_in_hbm(words):
    return words[0].rearrange("p n t -> p (n t)").bitcast(I32)


def load_scale_rows(queues, plane, scales):
    rows = scales[0].bitcast(I32)
    for q, queue in enumerate(queues):
        queue.dma_start(plane[32 * q : 32 * q + 4, :].bitcast(I32), rows[4 * q : 4 * q + 4, :])


def close_up(queues, plane, apart):
    for s, queue in enumerate(queues):
        queue.dma_start(plane[s:P:32, :].bitcast(I32), apart[8 * s : P : 32, :].bitcast(I32))


def deal_words(nc, dealt, plain):
    nc.vector.tensor_copy(
        dealt[:].rearrange("p (t c i) -> p c t i", t=PACK, i=4),
        plain[:].rearrange("p (c i t) -> p c t i", t=PACK, i=4),
    )


def deal_bytes(nc, dealt, plain, tiles=slice(0, PACK)):
    nc.vector.tensor_copy(
        dealt[:].rearrange("p (t m) -> p t m", t=PACK)[:, tiles, :],
        plain[:].rearrange("p (m t) -> p t m", t=PACK)[:, tiles, :],
    )


def product(nc, bank, t, w_words, w_scales, x_words, x_scales, places=slice(0, S)):
    cols = slice(t * P, (t + 1) * P)
    nc.tensor.matmul_mx(
        out=bank[:, places],
        lhsT=w_words[:, cols].bitcast(FP8X4),
        lhsT_scale=w_scales[:, cols],
        rhs=x_words[:, places].bitcast(FP8X4),
        rhs_scale=x_scales[:, places],
        start=True,
        stop=True,
    )


def round_pair(copy, grouped, planes, first, cols):
    copy(
        grouped[:, cols, first : first + 2],
        planes[:, first : first + 2, cols].rearrange("p t c -> p c t"),
    )


def quantise(nc, words, scales, grouped, cols):
    nc.vector.quantize_mx(
        words[:, cols].bitcast(FP8X4), scales[:, cols], grouped[:, cols, :].rearrange("p c t -> p (c t)")
    )


def tile_picked_cdjoinmaxbsendg_none_po_kernel(
    tc, x_words, x_scales, w1_words, w1_scales, gn, w2_words, w2_scales, d_words, d_scales,
    offs, n1, n2, two, k1, n3, n4, out_0, out_1, out_2,
):
    nc = tc.nc
    with ExitStack() as ctx:
        sb = ctx.enter_context(tc.tile_pool(name="sb", bufs=1))
        psum = ctx.enter_context(tc.psum_pool(name="psum", bufs=1))

        def tile(name, shape, dtype, tag=None):
            return sb.tile(shape, dtype, name=name, tag=tag or name, align_bytes=64)

        def load_list(name, src):
            lst = tile(name, list(src.shape), U16)
            nc.sync.dma_start(lst[:], src)
            return lst

        xw = tile("xw", [P, T], U32)
        xs = tile("xs", [P, T], U8)
        dw = tile("dw", [P, G], U32)
        dsc = tile("dsc", [P, G], U8)
        w1w = tile("w1w", [P, H], U32)
        w1s = tile("w1s", [P, H], U8)
        d_plane = tile("d_plane", [P, H], U8)
        gain = tile("gain", [P, PACK], F32)
        y = [tile(f"y{t}", [P, S + PAD], F32) for t in range(PACK)]

        xs_apart = tile("xs_apart", [P, T], U8)
        xq_plane = tile("xq_plane", [P, S], U8)
        for plane in (w1s, xs_apart, xq_plane, dsc, xs, d_plane):
            nc.vector.memset(plane[:].bitcast(I32), 0)
        for t in range(PACK):
            nc.vector.memset(y[t][:, S:], 0.0)

        offs_t = load_list("offs_t", offs)
        nc.sync.dma_start(w1w[:].bitcast(I32), words_in_hbm(w1_words))
        nc.sync.dma_start(xs_apart[0:P:8, :].bitcast(I32), x_scales[0].bitcast(I32))
        nc.sync.dma_start(xw[:].bitcast(I32), words_in_hbm(x_words))
        load_scale_rows([nc.scalar] * 4, w1s, w1_scales)
        n2_t = load_list("n2_t", n2)

        xq_s = tile("xq_s", [P, S], U8)
        xq_w = tile("xq_w", [P, S], U32)
        nc.vector.tensor_copy(xq_s[:], xs_apart[:].indirect(offs_t[:]))
        close_up([nc.scalar, nc.sync] * 2, xq_plane, xq_s)
        w1w_d = tile("w1w_d", [P, H], U32, tag="xs_apart")
        w1s_d = tile("w1s_d", [P, H], U8)
        deal_words(nc, w1w_d, w1w)
        deal_bytes(nc, w1s_d, w1s)
        nc.vector.tensor_copy(xq_w[:], xw[:].indirect(offs_t[:]))

        two_t = load_list("two_t", two)
        nc.sync.dma_start(dsc[0:P:8, :].bitcast(I32), d_scales[0].bitcast(I32))
        k1_t = load_list("k1_t", k1)
        nc.sync.dma_start(dw[:].bitcast(I32), words_in_hbm(d_words))
        n1_t = load_list("n1_t", n1)
        load_scale_rows([nc.sync] * 4, xs, x_scales)

        y_bank = [psum.tile([P, S], F32, name=f"y_bank{t}", tag=f"bank{t}") for t in range(PACK)]
        last = PACK - 1
        for t in (0, last, 1, 2):
            product(nc, y_bank[t], t, w1w_d, w1s_d, xq_w, xq_plane)

        b_sig = [tile(f"b_sig{t}", [P, 2 * S], F32) for t in range(PACK)]
        a_bg = [tile(f"a_bg{t}", [P, 2 * S], F32) for t in range(PACK)]
        yg = [tile(f"yg{t}", [P, S], F32) for t in range(PACK)]
        sm = tile("sm", [P, PACK, S], F32)
        ds = [tile(f"ds{t}", [P, 2 * S], F32) for t in range(PACK)]
        z = tile("z", [P, PACK, S], F32)
        zb = tile("zb", [P, S, PACK], BF16)

        nc.scalar.activation(b_sig[last][:, S:], y_bank[last][:], ACT.Sigmoid)
        for t in range(PACK):
            nc.vector.tensor_copy(y[t][:, :S], y_bank[t][:])
        for t in range(last):
            nc.scalar.activation(yg[t][:], y[t][:].indirect(n2_t[:]), ACT.Copy)
        for t in range(last):
            nc.scalar.activation(b_sig[t][:, S:], y[t][:, :S], ACT.Sigmoid)
        nc.scalar.activation(yg[last][:], y[last][:].indirect(n2_t[:]), ACT.Copy)

        dq_s = tile("dq_s", [P, H], U8)
        dq_s_d = tile("dq_s_d", [P, H], U8)
        nc.vector.tensor_copy(dq_s[:], dsc[:].indirect(k1_t[:]))
        deal_bytes(nc, dq_s_d, dq_s)
        close_up([nc.sync] * 4, d_plane, dq_s_d)
        nc.sync.dma_start(w1w[:].bitcast(I32), words_in_hbm(w2_words))
        load_scale_rows([nc.sync] * 4, w1s, w2_scales)
        nc.sync.dma_start(gain[:], gn.rearrange("(p t) o -> p (t o)", t=PACK))
        n4_t = load_list("n4_t", n4)
        n3_t = load_list("n3_t", n3)

        for t in range(PACK):
            nc.vector.tensor_tensor(sm[:, t, :], y[t][:, :S], yg[t][:], ALU.max)
        for t in range(PACK):
            nc.scalar.activation(ds[t][:].indirect(n1_t[:]), sm[:, t, :], ACT.Copy)

        dq_w = tile("dq_w", [P, H], U32, tag="yg2")
        dq_w_d = tile("dq_w_d", [P, H], U32)
        x2_s = tile("x2_s", [P, S], U8, tag="yg1")
        x2_w = tile("x2_w", [P, S], U32, tag="yg0")
        nc.vector.tensor_copy(x2_s[:], xs[:].indirect(two_t[:]))
        nc.vector.tensor_copy(x2_w[:], xw[:].indirect(two_t[:]))
        nc.vector.tensor_copy(dq_w[:], dw[:].indirect(k1_t[:]))
        deal_words(nc, dq_w_d, dq_w)
        w2w_d = tile("w2w_d", [P, N], U32)
        w2s_d = tile("w2s_d", [P, N], U8)
        deal_words(nc, w2w_d, w1w)
        deal_bytes(nc, w2s_d, w1s)
        b_bank = [psum.tile([P, S], F32, name=f"b_bank{t}") for t in range(PACK)]
        for t in range(PACK):
            product(nc, b_bank[t], t, dq_w_d, d_plane, x2_w, x2_s)
            nc.vector.tensor_scalar_mul(b_sig[t][:, :S], b_bank[t][:], 0.0625)

        def gated(t, cols):
            nc.vector.scalar_tensor_tensor(
                z[:, t, cols], ds[t][:, cols], gain[:, t : t + 1], b_sig[t][:, S:][:, cols], ALU.mult, ALU.mult
            )

        zw = tile("zw", [P, S], U32)
        zs = tile("zs", [P, S], U8)
        gated(0, ALL)
        gated(1, ALL)
        round_pair(nc.vector.tensor_copy, zb, z, 0, ALL)
        gated(2, ALL)
        for cols in HALVES:
            gated(3, cols)
        for cols in HALVES:
            round_pair(nc.vector.tensor_copy, zb, z, 2, cols)
        for cols in HALVES:
            quantise(nc, zw, zs, zb, cols)

        def fetch_b(t):
            nc.scalar.activation(a_bg[t][:, S:], b_sig[t][:].indirect(n4_t[:]), ACT.Copy)

        for t in range(PACK):
            fetch_b(t)

        a_bank = [psum.tile([P, S], F32, name=f"a_bank{t}", tag=f"bank{t}") for t in range(PACK)]
        for cols in HALVES:
            for t in (0, 1):
                product(nc, a_bank[t], t, w2w_d, w2s_d, zw, zs, cols)
        for t in (2, 3):
            product(nc, a_bank[t], t, w2w_d, w2s_d, zw, zs)

        hi = tile("hi", [P, PACK, S], F32)
        lo = tile("lo", [P, PACK, S], F32)
        ag = tile("ag", [P, PACK, S], F32)
        res = tile("res", [P, PACK, S], F32)
        rb = tile("rb", [P, S, PACK], BF16)
        ow = tile("ow", [P, S], U32)
        os_ = tile("os_", [P, S], U8)
        out_rows = out_0.rearrange("(p t) c -> p t c", t=PACK)
        first, second = HALVES

        def leave_bank(copy, t):
            copy(a_bg[t][:, :S], a_bank[t][:])

        def fetch_a(t, cols):
            entries = n3_t[:, cols.start // 16 : cols.stop // 16]
            nc.scalar.activation(ag[:, t, cols], a_bg[t][:].indirect(entries), ACT.Copy)

        def larger(t):
            nc.vector.tensor_tensor(hi[:, t, :], a_bank[t][:], a_bg[t][:, S:], ALU.max)

        def smaller(t, cols):
            nc.vector.scalar_tensor_tensor(lo[:, t, cols], b_bank[t][:, cols], 0.0625, ag[:, t, cols], ALU.mult, ALU.min)

        def less(t, cols, engine=nc.vector):
            engine.tensor_tensor(res[:, t, cols], hi[:, t, cols], lo[:, t, cols], ALU.subtract)

        for t in range(last):
            leave_bank(nc.vector.tensor_copy, t)
        fetch_a(0, ALL)
        leave_bank(nc.scalar.copy, last)
        fetch_a(1, ALL)
        for cols in HALVES:
            fetch_a(2, cols)
            fetch_a(3, cols)
        for t in range(last):
            larger(t)
        smaller(0, ALL)
        larger(last)
        less(0, ALL)
        smaller(1, ALL)
        less(1, ALL)
        nc.sync.dma_start(out_rows[:, 0:2, :], res[:, 0:2, :])
        round_pair(nc.scalar.copy, rb, res, 0, ALL)
        for cols in HALVES:
            smaller(2, cols)
            smaller(3, cols)
            less(2, cols)
            less(3, cols)
            nc.sync.dma_start(out_rows[:, 2:4, cols], res[:, 2:4, cols])
            round_pair(nc.vector.tensor_copy, rb, res, 2, cols)
        for cols in HALVES:
            quantise(nc, ow, os_, rb, cols)
            nc.sync.dma_start(words_in_hbm(out_1)[:, cols], ow[:, cols].bitcast(I32))
        rows = out_2[0].bitcast(I32)
        for q in range(4):
            queue = nc.scalar if q < 2 else nc.sync
            queue.dma_start(rows[4 * q : 4 * q + 4, :], os_[32 * q : 32 * q + 4, :].bitcast(I32))
